import numpy as np
import ml_dtypes


def mxq(x, axis, fmt="e4m3"):
    dtype, down = {"e4m3": (ml_dtypes.float8_e4m3fn, 7), "e5m2": (ml_dtypes.float8_e5m2, 14)}[fmt]
    v = np.moveaxis(np.asarray(x, np.float32).astype(ml_dtypes.bfloat16).astype(np.float64), axis, -1)
    blocks = v.reshape(v.shape[:-1] + (-1, 32))
    amax = np.abs(blocks).max(-1, keepdims=True)
    byte = np.maximum(np.where(amax > 0, np.frexp(amax)[1] - 1 + 127, 0) - down, 1)
    scale = np.exp2(byte - 127.0)
    codes = (blocks / scale).astype(np.float32).astype(dtype).astype(np.float64)
    return np.moveaxis((codes * scale).reshape(v.shape), -1, axis)


WIDE = False


def mx_kscale(k):
    if not WIDE:
        return np.ones(k)
    levels = np.array([30, -30])
    if k % 512:
        return np.exp2(np.random.permutation(np.resize(levels, k // 32))).repeat(32)
    a = np.empty((k // 512, 16))
    for p in range(k // 512):
        a[p, :8] = np.random.permutation(np.resize(levels, 8))
        for g in range(8):
            far = levels[np.abs(levels - a[p, g]) >= 10]
            a[p, g + 8] = far[np.random.randint(len(far))]
    return np.exp2(a.ravel()).repeat(32)


def f64(x):
    return np.asarray(x).astype(np.float64)


def striped(idx):
    return np.tile(np.asarray(idx).reshape(-1, 16).T, (8, 1)).astype(np.uint16)


def unstriped(offs):
    return offs[:16].T.reshape(-1).astype(np.int64)


E2M1 = np.array([0.0, 0.5, 1.0, 1.5, 2.0, 3.0, 4.0, 6.0, -0.0, -0.5, -1.0, -1.5, -2.0, -3.0, -4.0, -6.0])


def pack_weight(w, fmt):
    k, n = w.shape
    w = f64(np.asarray(w, np.float32).astype(ml_dtypes.bfloat16)).reshape(k // 32, 32, n)
    amax = np.abs(w).max(1)
    if fmt in ("e4m3", "e5m2"):
        byte = np.frexp(amax)[1] - 1 + 127 - (7 if fmt == "e4m3" else 14)
    else:
        mant, ex = np.frexp(amax / 6.0)
        byte = np.where(mant > 0.5, ex, ex - 1) + 127
    byte = np.clip(np.where(amax > 0, byte, 1), 1, 254)
    scaled = (w * np.exp2(127.0 - byte)[:, None, :]).reshape(k, n).astype(np.float32)
    by_word = np.ascontiguousarray(scaled.reshape(k // 512, 128, 4, n).transpose(0, 1, 3, 2))
    if fmt in ("e4m3", "e5m2"):
        words = by_word.astype(ml_dtypes.float8_e4m3fn if fmt == "e4m3" else ml_dtypes.float8_e5m2).view(np.uint8)
    else:
        c = by_word.astype(ml_dtypes.float4_e2m1fn).view(np.uint8) & 0xF
        words = (c[..., 0::2] | (c[..., 1::2] << 4)).reshape(k // 512, 128, 2 * n)
    return np.ascontiguousarray(words), np.ascontiguousarray(byte.astype(np.uint8).reshape(k // 512, 16, n))


def unpack_weight(words, scales, fmt):
    g, _, n = scales.shape
    words = np.ascontiguousarray(words).reshape(g, 128, n, -1)
    if fmt in ("e4m3", "e5m2"):
        vals = words.view(ml_dtypes.float8_e4m3fn if fmt == "e4m3" else ml_dtypes.float8_e5m2).astype(np.float64)
    else:
        nib = np.empty((g, 128, n, 4), np.uint8)
        nib[..., 0::2] = words & 0xF
        nib[..., 1::2] = words >> 4
        vals = E2M1[nib]
    vals = vals * np.repeat(np.exp2(scales.astype(np.float64) - 127.0), 8, axis=1)[..., None]
    return vals.transpose(0, 1, 3, 2).reshape(g * 512, n)


K, T, Z, J, R, C, O, N, L, E = 512, 1024, 1024, 256, 512, 512, 256, 256, 512, 1024


def setup_inputs():
    n = np.random.standard_normal
    idx = np.random.permutation(T)[:J]
    idx2 = np.random.permutation(Z)[:J]
    idx3 = np.random.permutation(C)[:J]
    idx4 = np.random.permutation(C)[:J]
    idx5 = np.random.permutation(C)[:O]
    idx6 = np.random.permutation(C)[:O]
    idx7 = np.random.permutation(E)[:O]
    fk = mx_kscale(K)
    fr = mx_kscale(R)
    fl = mx_kscale(L)
    xtp = pack_weight(n((K, T)) / fk[:, None], "e5m2")
    xop = pack_weight(n((K, Z)) / fk[:, None], "e4m3")
    wp = pack_weight(n((K, R)) * 1 / np.sqrt(K) * fk[:, None] * fr, "e2m1")
    wbp = pack_weight(n((R, N)) * 1 / np.sqrt(R) / fr[:, None], "e2m1")
    sxp = pack_weight(n((L, O)) / fl[:, None], "e4m3")
    wsp = pack_weight(n((L, N)) * 1 / np.sqrt(L) * fl[:, None], "e2m1")
    return {
        "xt_words": xtp[0],
        "xt_scales": xtp[1],
        "xo_words": xop[0],
        "xo_scales": xop[1],
        "w_words": wp[0],
        "w_scales": wp[1],
        "wb_words": wbp[0],
        "wb_scales": wbp[1],
        "sx_words": sxp[0],
        "sx_scales": sxp[1],
        "ws_words": wsp[0],
        "ws_scales": wsp[1],
        "offs": striped(idx),
        "offs2": striped(idx2),
        "offs3": striped(idx3),
        "offs4": striped(idx4),
        "offs5": striped(idx5),
        "offs6": striped(idx6),
        "offs7": striped(idx7),
    }


def reference(xt_words, xt_scales, xo_words, xo_scales, w_words, w_scales, wb_words, wb_scales, sx_words, sx_scales, ws_words, ws_scales, offs, offs2, offs3, offs4, offs5, offs6, offs7):
    idx = unstriped(offs)
    idx2 = unstriped(offs2)
    idx3 = unstriped(offs3)
    idx4 = unstriped(offs4)
    idx5 = unstriped(offs5)
    idx6 = unstriped(offs6)
    idx7 = unstriped(offs7)
    xtu = unpack_weight(xt_words, xt_scales, "e5m2")
    xou = unpack_weight(xo_words, xo_scales, "e4m3")
    wu = unpack_weight(w_words, w_scales, "e2m1")
    wbu = unpack_weight(wb_words, wb_scales, "e2m1")
    sxu = unpack_weight(sx_words, sx_scales, "e4m3")
    wsu = unpack_weight(ws_words, ws_scales, "e2m1")
    xtidxg = xtu[:, idx]
    a = wu.T @ xtidxg
    xoidx2g = xou[:, idx2]
    b = wu.T @ xoidx2g
    pw = np.zeros((R, C))
    pw[:, idx3] = a
    pv = np.zeros((R, C))
    pv[:, idx4] = b
    hid = np.abs(pw[:, idx5] - pv[:, idx6])
    hidq = mxq(hid, 0, "e4m3")
    p = wbu.T @ hidq + wsu.T @ sxu
    y = np.zeros((N, E))
    y[:, idx7] = p
    return y

@@ -1,0 +1,176 @@
+from contextlib import ExitStack
+
+import concourse.mybir as mybir
+
+K, T, Z, J, R, C, O, N, L, E = 512, 1024, 1024, 256, 512, 512, 256, 256, 512, 1024
+FLOPS = 2 * K * R * J * 2 + 2 * R * N * O + 2 * L * N * O
+
+F32 = mybir.dt.float32
+BF16 = mybir.dt.bfloat16
+I32 = mybir.dt.int32
+U32 = mybir.dt.uint32
+U16 = mybir.dt.uint16
+U8 = mybir.dt.uint8
+E4M3 = mybir.dt.float8_e4m3fn_x4
+E5M2 = mybir.dt.float8_e5m2_x4
+E2M1 = mybir.dt.float4_e2m1fn_x4
+ACT = mybir.ActivationFunctionType
+ALU = mybir.AluOpType
+
+P = 128
+PACK = 4
+
+
+def tile_list_oneforboth_twoboards_skip_scattered_kernel(
+    tc, xt_words, xt_scales, xo_words, xo_scales, w_words, w_scales, wb_words, wb_scales,
+    sx_words, sx_scales, ws_words, ws_scales, offs, offs2, offs3, offs4, offs5, offs6, offs7, out,
+):
+    nc = tc.nc
+    with ExitStack() as ctx:
+        lists = ctx.enter_context(tc.tile_pool(name="lists", bufs=1))
+        keep = ctx.enter_context(tc.tile_pool(name="keep", bufs=1))
+        psum = ctx.enter_context(tc.psum_pool(name="psum", bufs=1))
+
+        def load_list(name, src):
+            tile = lists.tile([P, 16], U16, name=name)
+            nc.sync.dma_start(tile[:], src)
+            return tile
+
+        def load_fp8_words(name, src, width):
+            tile = keep.tile([P, width], U32, name=name, align_bytes=64)
+            nc.sync.dma_start(tile[:].bitcast(I32), src[0].rearrange("p c r -> p (c r)").bitcast(I32))
+            return tile
+
+        def load_fp4_words(name, src, width):
+            tile = keep.tile([P, 2 * width], U8, name=name, align_bytes=64)
+            nc.sync.dma_start(tile[:].bitcast(I32), src[0].bitcast(I32))
+            return tile
+
+        def load_scales(name, src, width, clear, queue):
+            tile = keep.tile([P, width], U8, name=name, align_bytes=64)
+            clear.memset(tile[:].bitcast(I32), 0)
+            for q in range(4):
+                queue.dma_start(tile[32 * q : 32 * q + 4, :].bitcast(I32), src[0, 4 * q : 4 * q + 4, :].bitcast(I32))
+            return tile
+
+
+        tok_list = load_list("tok_list", offs)
+        w_raw = load_fp4_words("w_raw", w_words, R)
+        xt_sc = load_scales("xt_sc", xt_scales, T, nc.vector, nc.sync)
+        xt_w = load_fp8_words("xt_w", xt_words, T)
+        w_raw_sc = load_scales("w_raw_sc", w_scales, R, nc.vector, nc.sync)
+        put_a = load_list("put_a", offs3)
+        xo_w = load_fp8_words("xo_w", xo_words, Z)
+        note_list = load_list("note_list", offs2)
+        xo_sc = load_scales("xo_sc", xo_scales, Z, nc.vector, nc.sync)
+        put_b = load_list("put_b", offs4)
+        read_a = load_list("read_a", offs5)
+        read_b = load_list("read_b", offs6)
+        sx_w = load_fp8_words("sx_w", sx_words, O)
+        sx_sc = load_scales("sx_sc", sx_scales, O, nc.vector, nc.sync)
+        ws_w = load_fp4_words("ws_w", ws_words, N)
+        ws_sc = load_scales("ws_sc", ws_scales, N, nc.vector, nc.sync)
+        wb_w = load_fp4_words("wb_w", wb_words, N)
+        wb_sc = load_scales("wb_sc", wb_scales, N, nc.vector, nc.sync)
+        put_p = load_list("put_p", offs7)
+
+        pw = [keep.tile([P, C], F32, name="pw%d" % t) for t in range(PACK)]
+        pv = [keep.tile([P, C], F32, name="pv%d" % t) for t in range(PACK)]
+        pages = [keep.tile([P, E], F32, name="page%d" % h) for h in range(N // P)]
+        for t in range(PACK):
+            nc.vector.memset(pw[t][:], 0.0)
+        for t in range(PACK):
+            nc.gpsimd.memset(pv[t][:], 0.0)
+        for page in pages:
+            nc.gpsimd.memset(page[:], 0.0)
+
+        w_w = keep.tile([P, PACK, P, 2], U8, name="w_w", align_bytes=64)
+        nc.vector.tensor_copy(w_w[:], w_raw[:].rearrange("p (m t b) -> p t m b", t=PACK, b=2))
+        w_sc = keep.tile([P, PACK, P], U8, name="w_sc", align_bytes=64)
+        nc.vector.tensor_copy(w_sc[:], w_raw_sc[:].rearrange("p (m t) -> p t m", t=PACK))
+
+        def pick(name, words, scales, offsets):
+            picked_sc = keep.tile([P, J], U8, name=name + "_sc", align_bytes=64)
+            nc.vector.tensor_copy(picked_sc[:], scales[:].indirect(offsets[:]))
+            picked_w = keep.tile([P, J], U32, name=name + "_w", align_bytes=64)
+            nc.vector.tensor_copy(picked_w[:], words[:].indirect(offsets[:]))
+            return picked_w, picked_sc
+
+        def first_product(name, picked_w, picked_sc, fmt):
+            banks = [psum.tile([P, 2, J], F32, name="%s_bank%d" % (name, u)) for u in range(2)]
+            for t in range(PACK):
+                nc.tensor.matmul_mx(
+                    out=banks[t // 2][:, t % 2, :],
+                    lhsT=w_w[:, t].rearrange("p m b -> p (m b)").bitcast(E2M1),
+                    lhsT_scale=w_sc[:, t, :],
+                    rhs=picked_w[:].bitcast(fmt),
+                    rhs_scale=picked_sc[:],
+                    start=True,
+                    stop=True,
+                )
+            return banks
+
+        a_sb = [keep.tile([P, 2, J], F32, name="a_sb%d" % u) for u in range(2)]
+        b_sb = [keep.tile([P, 2, J], F32, name="b_sb%d" % u) for u in range(2)]
+        got_a = [keep.tile([P, O], F32, name="got_a%d" % t) for t in range(PACK)]
+        diff = keep.tile([P, PACK, O], F32, name="diff")
+
+        def place_pair(board, sums, offsets, u):
+            for t in (2 * u, 2 * u + 1):
+                if u == 0:
+                    nc.vector.tensor_copy(board[t][:].indirect(offsets[:]), sums[u][:, t % 2, :])
+                else:
+                    nc.scalar.activation(board[t][:].indirect(offsets[:]), sums[u][:, t % 2, :], ACT.Copy)
+
+        tok_w, tok_sc = pick("tok", xt_w, xt_sc, tok_list)
+        a_banks = first_product("a", tok_w, tok_sc, E5M2)
+        nc.vector.tensor_copy(a_sb[0][:], a_banks[0][:])
+        nc.scalar.copy(a_sb[1][:], a_banks[1][:])
+        note_w, note_sc = pick("note", xo_w, xo_sc, note_list)
+        b_banks = first_product("b", note_w, note_sc, E4M3)
+        place_pair(pw, a_sb, put_a, 0)
+        place_pair(pw, a_sb, put_a, 1)
+        for u in range(2):
+            nc.scalar.copy(b_sb[u][:], b_banks[u][:])
+        place_pair(pv, b_sb, put_b, 0)
+        for t in range(PACK):
+            nc.scalar.activation(got_a[t][:], pw[t][:].indirect(read_a[:]), ACT.Copy)
+        place_pair(pv, b_sb, put_b, 1)
+        for t in range(PACK):
+            nc.vector.tensor_tensor(diff[:, t, :], pv[t][:].indirect(read_b[:]), got_a[t][:], ALU.subtract)
+
+        p_banks = [psum.tile([P, O], F32, name="p_bank%d" % h) for h in range(N // P)]
+        for h in range(N // P):
+            nc.tensor.matmul_mx(
+                out=p_banks[h][:],
+                lhsT=ws_w[:, 2 * P * h : 2 * P * (h + 1)].bitcast(E2M1),
+                lhsT_scale=ws_sc[:, P * h : P * (h + 1)],
+                rhs=sx_w[:].bitcast(E4M3),
+                rhs_scale=sx_sc[:],
+                start=True,
+                stop=False,
+            )
+
+        hid = keep.tile([P, O, PACK], BF16, name="hid", align_bytes=64)
+        nc.scalar.activation(hid[:], diff[:].rearrange("p t o -> p o t"), ACT.Abs)
+        hid_w = keep.tile([P, O], U32, name="hid_w", align_bytes=64)
+        hid_sc = keep.tile([P, O], U8, name="hid_sc", align_bytes=64)
+        nc.vector.quantize_mx(out=hid_w[:].bitcast(E4M3), scales=hid_sc[:], in_=hid[:].rearrange("p o t -> p (o t)"))
+
+        p_sb = [keep.tile([P, O], F32, name="p_sb%d" % h) for h in range(N // P)]
+        for h in range(N // P):
+            nc.tensor.matmul_mx(
+                out=p_banks[h][:],
+                lhsT=wb_w[:, 2 * P * h : 2 * P * (h + 1)].bitcast(E2M1),
+                lhsT_scale=wb_sc[:, P * h : P * (h + 1)],
+                rhs=hid_w[:].bitcast(E4M3),
+                rhs_scale=hid_sc[:],
+                start=False,
+                stop=True,
+            )
+        nc.vector.tensor_copy(p_sb[0][:], p_banks[0][:])
+        nc.vector.tensor_copy(pages[0][:].indirect(put_p[:]), p_sb[0][:])
+        nc.sync.dma_start(out[0:P, :], pages[0][:])
+        nc.scalar.copy(p_sb[1][:], p_banks[1][:])
+        nc.scalar.activation(pages[1][:].indirect(put_p[:]), p_sb[1][:], ACT.Copy)
+        nc.sync.dma_start(out[P : 2 * P, :], pages[1][:])

@@ -37,7 +37,7 @@ def tile_list_oneforboth_twoboards_skip_scattered_kernel(
             return tile
 
         def load_fp8_words(name, src, width):
-            tile = keep.tile([P, width], U32, name=name, align_bytes=64)
+            tile = keep.tile([P, width], U32, name=name, tag=name, align_bytes=64)
             nc.sync.dma_start(tile[:].bitcast(I32), src[0].rearrange("p c r -> p (c r)").bitcast(I32))
             return tile
 
@@ -59,10 +59,10 @@ def tile_list_oneforboth_twoboards_skip_scattered_kernel(
         xt_sc = load_scales("xt_sc", xt_scales, T, nc.vector, nc.sync)
         xt_w = load_fp8_words("xt_w", xt_words, T)
         w_raw_sc = load_scales("w_raw_sc", w_scales, R, nc.vector, nc.sync)
-        put_a = load_list("put_a", offs3)
-        xo_w = load_fp8_words("xo_w", xo_words, Z)
         note_list = load_list("note_list", offs2)
+        xo_w = load_fp8_words("xo_w", xo_words, Z)
         xo_sc = load_scales("xo_sc", xo_scales, Z, nc.vector, nc.sync)
+        put_a = load_list("put_a", offs3)
         put_b = load_list("put_b", offs4)
         read_a = load_list("read_a", offs5)
         read_b = load_list("read_b", offs6)
@@ -76,68 +76,72 @@ def tile_list_oneforboth_twoboards_skip_scattered_kernel(
 
         pw = [keep.tile([P, C], F32, name="pw%d" % t) for t in range(PACK)]
         pv = [keep.tile([P, C], F32, name="pv%d" % t) for t in range(PACK)]
-        pages = [keep.tile([P, E], F32, name="page%d" % h) for h in range(N // P)]
-        for t in range(PACK):
-            nc.vector.memset(pw[t][:], 0.0)
-        for t in range(PACK):
-            nc.gpsimd.memset(pv[t][:], 0.0)
-        for page in pages:
-            nc.gpsimd.memset(page[:], 0.0)
 
-        w_w = keep.tile([P, PACK, P, 2], U8, name="w_w", align_bytes=64)
-        nc.vector.tensor_copy(w_w[:], w_raw[:].rearrange("p (m t b) -> p t m b", t=PACK, b=2))
-        w_sc = keep.tile([P, PACK, P], U8, name="w_sc", align_bytes=64)
-        nc.vector.tensor_copy(w_sc[:], w_raw_sc[:].rearrange("p (m t) -> p t m", t=PACK))
+        w_w = keep.tile([P, PACK, 2 * P], U8, name="w_w", align_bytes=64)
+        nc.vector.tensor_copy(w_w[:].bitcast(U16), w_raw[:].bitcast(U16).rearrange("p (m t) -> p t m", t=PACK))
 
-        def pick(name, words, scales, offsets):
-            picked_sc = keep.tile([P, J], U8, name=name + "_sc", align_bytes=64)
-            nc.vector.tensor_copy(picked_sc[:], scales[:].indirect(offsets[:]))
-            picked_w = keep.tile([P, J], U32, name=name + "_w", align_bytes=64)
-            nc.vector.tensor_copy(picked_w[:], words[:].indirect(offsets[:]))
-            return picked_w, picked_sc
+        def pick(name, table, offsets, dtype, tag):
+            picked = keep.tile([P, J], dtype, name=name, tag=tag, align_bytes=64)
+            nc.vector.tensor_copy(picked[:], table[:].indirect(offsets[:]))
+            return picked
 
-        def first_product(name, picked_w, picked_sc, fmt):
-            banks = [psum.tile([P, 2, J], F32, name="%s_bank%d" % (name, u)) for u in range(2)]
-            for t in range(PACK):
+        def first_product(sums, picked_w, picked_sc, fmt, order):
+            for t in order:
                 nc.tensor.matmul_mx(
-                    out=banks[t // 2][:, t % 2, :],
-                    lhsT=w_w[:, t].rearrange("p m b -> p (m b)").bitcast(E2M1),
+                    out=sums[t],
+                    lhsT=w_w[:, t, :].bitcast(E2M1),
                     lhsT_scale=w_sc[:, t, :],
                     rhs=picked_w[:].bitcast(fmt),
                     rhs_scale=picked_sc[:],
                     start=True,
                     stop=True,
                 )
-            return banks
 
-        a_sb = [keep.tile([P, 2, J], F32, name="a_sb%d" % u) for u in range(2)]
+        a_sb = [keep.tile([P, J], F32, name="a_sb%d" % t) for t in range(PACK)]
         b_sb = [keep.tile([P, 2, J], F32, name="b_sb%d" % u) for u in range(2)]
         got_a = [keep.tile([P, O], F32, name="got_a%d" % t) for t in range(PACK)]
-        diff = keep.tile([P, PACK, O], F32, name="diff")
+        diff = [keep.tile([P, 2, O], F32, name="diff%d" % u) for u in range(2)]
 
-        def place_pair(board, sums, offsets, u):
-            for t in (2 * u, 2 * u + 1):
-                if u == 0:
-                    nc.vector.tensor_copy(board[t][:].indirect(offsets[:]), sums[u][:, t % 2, :])
-                else:
-                    nc.scalar.activation(board[t][:].indirect(offsets[:]), sums[u][:, t % 2, :], ACT.Copy)
+        def place(board, values, offsets, t):
+            if t < 2:
+                nc.vector.tensor_copy(board[t][:].indirect(offsets[:]), values)
+            else:
+                nc.scalar.activation(board[t][:].indirect(offsets[:]), values, ACT.Copy)
 
-        tok_w, tok_sc = pick("tok", xt_w, xt_sc, tok_list)
-        a_banks = first_product("a", tok_w, tok_sc, E5M2)
+        tok_sc = pick("tok_sc", xt_sc, tok_list, U8, "picked_sc")
+        tok_w = pick("tok_w", xt_w, tok_list, U32, "picked_w")
+        w_sc = keep.tile([P, PACK, P], U8, name="w_sc", align_bytes=64)
+        nc.vector.tensor_copy(w_sc[:], w_raw_sc[:].rearrange("p (m t) -> p t m", t=PACK))
+        a_banks = [psum.tile([P, J], F32, name="a_bank%d" % t) for t in range(PACK)]
+        first_product([bank[:] for bank in a_banks], tok_w, tok_sc, E5M2, (0, 2, 1, 3))
+        for t in (0, 2, 1, 3):
+            nc.vector.memset(pw[t][:], 0.0)
+        for t in (0, 2, 1, 3):
+            nc.vector.memset(pv[t][:], 0.0)
         nc.vector.tensor_copy(a_sb[0][:], a_banks[0][:])
-        nc.scalar.copy(a_sb[1][:], a_banks[1][:])
-        note_w, note_sc = pick("note", xo_w, xo_sc, note_list)
-        b_banks = first_product("b", note_w, note_sc, E4M3)
-        place_pair(pw, a_sb, put_a, 0)
-        place_pair(pw, a_sb, put_a, 1)
+        note_w = pick("note_w", xo_w, note_list, U32, "picked_w")
+        note_sc = pick("note_sc", xo_sc, note_list, U8, "picked_sc")
+        b_banks = [psum.tile([P, 2, J], F32, name="b_bank%d" % u) for u in range(2)]
+        first_product([b_banks[t // 2][:, t % 2, :] for t in range(PACK)], note_w, note_sc, E4M3, range(PACK))
+        pages = [keep.tile([P, E], F32, name="page%d" % h, tag=tag, align_bytes=64) for h, tag in enumerate(("xt_w", "xo_w"))]
+        for page in pages:
+            nc.gpsimd.memset(page[:], 0.0)
+        place(pw, a_sb[0][:], put_a, 0)
+        nc.vector.tensor_copy(a_sb[1][:], a_banks[1][:])
+        place(pw, a_sb[1][:], put_a, 1)
+        for t in (2, 3):
+            nc.scalar.copy(a_sb[t][:], a_banks[t][:])
+            place(pw, a_sb[t][:], put_a, t)
         for u in range(2):
             nc.scalar.copy(b_sb[u][:], b_banks[u][:])
-        place_pair(pv, b_sb, put_b, 0)
+        for t in (0, 1):
+            place(pv, b_sb[t // 2][:, t % 2, :], put_b, t)
         for t in range(PACK):
             nc.scalar.activation(got_a[t][:], pw[t][:].indirect(read_a[:]), ACT.Copy)
-        place_pair(pv, b_sb, put_b, 1)
+        for t in (2, 3):
+            place(pv, b_sb[t // 2][:, t % 2, :], put_b, t)
         for t in range(PACK):
-            nc.vector.tensor_tensor(diff[:, t, :], pv[t][:].indirect(read_b[:]), got_a[t][:], ALU.subtract)
+            nc.vector.tensor_tensor(diff[t // 2][:, t % 2, :], pv[t][:].indirect(read_b[:]), got_a[t][:], ALU.subtract)
 
         p_banks = [psum.tile([P, O], F32, name="p_bank%d" % h) for h in range(N // P)]
         for h in range(N // P):
@@ -152,7 +156,17 @@ def tile_list_oneforboth_twoboards_skip_scattered_kernel(
             )
 
         hid = keep.tile([P, O, PACK], BF16, name="hid", align_bytes=64)
-        nc.scalar.activation(hid[:], diff[:].rearrange("p t o -> p o t"), ACT.Abs)
+        def magnitude_on_scalar(u, cols):
+            nc.scalar.activation(
+                hid[:, cols, 2 * u : 2 * u + 2].rearrange("p (c i) t -> p c t i", i=4),
+                diff[u][:, :, cols].rearrange("p t (c i) -> p c t i", i=4),
+                ACT.Abs,
+            )
+
+        magnitude_on_scalar(0, slice(0, O))
+        magnitude_on_scalar(1, slice(0, O // 2))
+        upper = diff[1][:, :, O // 2 :].rearrange("p t o -> p o t")
+        nc.vector.scalar_tensor_tensor(hid[:, O // 2 :, 2:4], upper, -1.0, upper, ALU.mult, ALU.max)
         hid_w = keep.tile([P, O], U32, name="hid_w", align_bytes=64)
         hid_sc = keep.tile([P, O], U8, name="hid_sc", align_bytes=64)
         nc.vector.quantize_mx(out=hid_w[:].bitcast(E4M3), scales=hid_sc[:], in_=hid[:].rearrange("p o t -> p (o t)"))

@@ -46,32 +46,39 @@ def tile_list_oneforboth_twoboards_skip_scattered_kernel(
             nc.sync.dma_start(tile[:].bitcast(I32), src[0].bitcast(I32))
             return tile
 
-        def load_scales(name, src, width, clear, queue):
-            tile = keep.tile([P, width], U8, name=name, align_bytes=64)
-            clear.memset(tile[:].bitcast(I32), 0)
-            for q in range(4):
-                queue.dma_start(tile[32 * q : 32 * q + 4, :].bitcast(I32), src[0, 4 * q : 4 * q + 4, :].bitcast(I32))
+        def cleared_plane(name, width):
+            tile = keep.tile([P, width], U8, name=name, tag=name, align_bytes=64)
+            nc.vector.memset(tile[:].bitcast(I32), 0)
             return tile
+
+        def load_scales(plane, first, src, width):
+            for q in range(4):
+                nc.sync.dma_start(
+                    plane[32 * q : 32 * q + 4, first : first + width].bitcast(I32),
+                    src[0, 4 * q : 4 * q + 4, :].bitcast(I32),
+                )
+            return plane[:, first : first + width]
 
 
         tok_list = load_list("tok_list", offs)
         w_raw = load_fp4_words("w_raw", w_words, R)
-        xt_sc = load_scales("xt_sc", xt_scales, T, nc.vector, nc.sync)
+        xt_sc = load_scales(cleared_plane("xt_sc", T), 0, xt_scales, T)
         xt_w = load_fp8_words("xt_w", xt_words, T)
-        w_raw_sc = load_scales("w_raw_sc", w_scales, R, nc.vector, nc.sync)
+        w_raw_sc = load_scales(cleared_plane("w_raw_sc", R), 0, w_scales, R)
         note_list = load_list("note_list", offs2)
         xo_w = load_fp8_words("xo_w", xo_words, Z)
-        xo_sc = load_scales("xo_sc", xo_scales, Z, nc.vector, nc.sync)
+        xo_sc = load_scales(cleared_plane("xo_sc", Z), 0, xo_scales, Z)
         put_a = load_list("put_a", offs3)
         put_b = load_list("put_b", offs4)
         read_a = load_list("read_a", offs5)
         read_b = load_list("read_b", offs6)
         sx_w = load_fp8_words("sx_w", sx_words, O)
-        sx_sc = load_scales("sx_sc", sx_scales, O, nc.vector, nc.sync)
+        second_planes = cleared_plane("second_planes", O + 2 * N)
+        sx_sc = load_scales(second_planes, 0, sx_scales, O)
         ws_w = load_fp4_words("ws_w", ws_words, N)
-        ws_sc = load_scales("ws_sc", ws_scales, N, nc.vector, nc.sync)
+        ws_sc = load_scales(second_planes, O, ws_scales, N)
         wb_w = load_fp4_words("wb_w", wb_words, N)
-        wb_sc = load_scales("wb_sc", wb_scales, N, nc.vector, nc.sync)
+        wb_sc = load_scales(second_planes, O + N, wb_scales, N)
         put_p = load_list("put_p", offs7)
 
         pw = [keep.tile([P, C], F32, name="pw%d" % t) for t in range(PACK)]
@@ -90,14 +97,14 @@ def tile_list_oneforboth_twoboards_skip_scattered_kernel(
                 nc.tensor.matmul_mx(
                     out=sums[t],
                     lhsT=w_w[:, t, :].bitcast(E2M1),
-                    lhsT_scale=w_sc[:, t, :],
+                    lhsT_scale=w_sc[t][:],
                     rhs=picked_w[:].bitcast(fmt),
                     rhs_scale=picked_sc[:],
                     start=True,
                     stop=True,
                 )
 
-        a_sb = [keep.tile([P, J], F32, name="a_sb%d" % t) for t in range(PACK)]
+        a_sb = [keep.tile([P, J], F32, name="a_sb%d" % t, tag="a_sb%d" % t, align_bytes=64) for t in range(PACK)]
         b_sb = [keep.tile([P, 2, J], F32, name="b_sb%d" % u) for u in range(2)]
         got_a = [keep.tile([P, O], F32, name="got_a%d" % t) for t in range(PACK)]
         diff = [keep.tile([P, 2, O], F32, name="diff%d" % u) for u in range(2)]
@@ -110,22 +117,22 @@ def tile_list_oneforboth_twoboards_skip_scattered_kernel(
 
         tok_sc = pick("tok_sc", xt_sc, tok_list, U8, "picked_sc")
         tok_w = pick("tok_w", xt_w, tok_list, U32, "picked_w")
-        w_sc = keep.tile([P, PACK, P], U8, name="w_sc", align_bytes=64)
-        nc.vector.tensor_copy(w_sc[:], w_raw_sc[:].rearrange("p (m t) -> p t m", t=PACK))
-        a_banks = [psum.tile([P, J], F32, name="a_bank%d" % t) for t in range(PACK)]
+        w_sc = [keep.tile([P, P], U8, name="w_sc%d" % t, align_bytes=64) for t in range(PACK)]
+        for t in (0, 2, 1, 3):
+            nc.vector.tensor_copy(w_sc[t][:], w_raw_sc[:, t::PACK])
+        a_banks = [psum.tile([P, J], F32, name="a_bank%d" % t, tag="bank%d" % t) for t in range(PACK)]
         first_product([bank[:] for bank in a_banks], tok_w, tok_sc, E5M2, (0, 2, 1, 3))
         for t in (0, 2, 1, 3):
             nc.vector.memset(pw[t][:], 0.0)
-        for t in (0, 2, 1, 3):
+        for t in range(PACK):
             nc.vector.memset(pv[t][:], 0.0)
+        page0 = keep.tile([P, E], F32, name="page0", tag="w_raw_sc", align_bytes=64)
+        nc.vector.memset(page0[:], 0.0)
         nc.vector.tensor_copy(a_sb[0][:], a_banks[0][:])
         note_w = pick("note_w", xo_w, note_list, U32, "picked_w")
         note_sc = pick("note_sc", xo_sc, note_list, U8, "picked_sc")
         b_banks = [psum.tile([P, 2, J], F32, name="b_bank%d" % u) for u in range(2)]
         first_product([b_banks[t // 2][:, t % 2, :] for t in range(PACK)], note_w, note_sc, E4M3, range(PACK))
-        pages = [keep.tile([P, E], F32, name="page%d" % h, tag=tag, align_bytes=64) for h, tag in enumerate(("xt_w", "xo_w"))]
-        for page in pages:
-            nc.gpsimd.memset(page[:], 0.0)
         place(pw, a_sb[0][:], put_a, 0)
         nc.vector.tensor_copy(a_sb[1][:], a_banks[1][:])
         place(pw, a_sb[1][:], put_a, 1)
@@ -155,7 +162,7 @@ def tile_list_oneforboth_twoboards_skip_scattered_kernel(
                 stop=False,
             )
 
-        hid = keep.tile([P, O, PACK], BF16, name="hid", align_bytes=64)
+        hid = keep.tile([P, O, PACK], BF16, name="hid", tag="hid", align_bytes=64)
         def magnitude_on_scalar(u, cols):
             nc.scalar.activation(
                 hid[:, cols, 2 * u : 2 * u + 2].rearrange("p (c i) t -> p c t i", i=4),
@@ -171,6 +178,9 @@ def tile_list_oneforboth_twoboards_skip_scattered_kernel(
         hid_sc = keep.tile([P, O], U8, name="hid_sc", align_bytes=64)
         nc.vector.quantize_mx(out=hid_w[:].bitcast(E4M3), scales=hid_sc[:], in_=hid[:].rearrange("p o t -> p (o t)"))
 
+        page1 = keep.tile([P, E], F32, name="page1", tag="hid", align_bytes=64)
+        nc.vector.memset(page1[:], 0.0)
+        pages = [page0, page1]
         p_sb = [keep.tile([P, O], F32, name="p_sb%d" % h) for h in range(N // P)]
         for h in range(N // P):
             nc.tensor.matmul_mx(

from contextlib import ExitStack

import concourse.mybir as mybir

K, T, Z, J, R, C, O, N, L, E = 512, 1024, 1024, 256, 512, 512, 256, 256, 512, 1024
FLOPS = 2 * K * R * J * 2 + 2 * R * N * O + 2 * L * N * O

F32 = mybir.dt.float32
BF16 = mybir.dt.bfloat16
I32 = mybir.dt.int32
U32 = mybir.dt.uint32
U16 = mybir.dt.uint16
U8 = mybir.dt.uint8
E4M3 = mybir.dt.float8_e4m3fn_x4
E5M2 = mybir.dt.float8_e5m2_x4
E2M1 = mybir.dt.float4_e2m1fn_x4
ACT = mybir.ActivationFunctionType
ALU = mybir.AluOpType

P = 128
PACK = 4


def tile_list_oneforboth_twoboards_skip_scattered_kernel(
    tc, xt_words, xt_scales, xo_words, xo_scales, w_words, w_scales, wb_words, wb_scales,
    sx_words, sx_scales, ws_words, ws_scales, offs, offs2, offs3, offs4, offs5, offs6, offs7, out,
):
    nc = tc.nc
    with ExitStack() as ctx:
        lists = ctx.enter_context(tc.tile_pool(name="lists", bufs=1))
        keep = ctx.enter_context(tc.tile_pool(name="keep", bufs=1))
        psum = ctx.enter_context(tc.psum_pool(name="psum", bufs=1))

        def load_list(name, src):
            tile = lists.tile([P, 16], U16, name=name)
            nc.sync.dma_start(tile[:], src)
            return tile

        def load_fp8_words(name, src, width):
            tile = keep.tile([P, width], U32, name=name, tag=name, align_bytes=64)
            nc.sync.dma_start(tile[:].bitcast(I32), src[0].rearrange("p c r -> p (c r)").bitcast(I32))
            return tile

        def load_fp4_words(name, src, width):
            tile = keep.tile([P, 2 * width], U8, name=name, align_bytes=64)
            nc.sync.dma_start(tile[:].bitcast(I32), src[0].bitcast(I32))
            return tile

        def cleared_plane(name, width):
            tile = keep.tile([P, width], U8, name=name, tag=name, align_bytes=64)
            nc.vector.memset(tile[:].bitcast(I32), 0)
            return tile

        def load_scales(plane, first, src, width):
            for q in range(4):
                nc.sync.dma_start(
                    plane[32 * q : 32 * q + 4, first : first + width].bitcast(I32),
                    src[0, 4 * q : 4 * q + 4, :].bitcast(I32),
                )
            return plane[:, first : first + width]


        tok_list = load_list("tok_list", offs)
        w_raw = load_fp4_words("w_raw", w_words, R)
        xt_sc = load_scales(cleared_plane("xt_sc", T), 0, xt_scales, T)
        xt_w = load_fp8_words("xt_w", xt_words, T)
        w_raw_sc = load_scales(cleared_plane("w_raw_sc", R), 0, w_scales, R)
        note_list = load_list("note_list", offs2)
        xo_w = load_fp8_words("xo_w", xo_words, Z)
        xo_sc = load_scales(cleared_plane("xo_sc", Z), 0, xo_scales, Z)
        put_a = load_list("put_a", offs3)
        put_b = load_list("put_b", offs4)
        read_a = load_list("read_a", offs5)
        read_b = load_list("read_b", offs6)
        sx_w = load_fp8_words("sx_w", sx_words, O)
        second_planes = cleared_plane("second_planes", O + 2 * N)
        sx_sc = load_scales(second_planes, 0, sx_scales, O)
        ws_w = load_fp4_words("ws_w", ws_words, N)
        ws_sc = load_scales(second_planes, O, ws_scales, N)
        wb_w = load_fp4_words("wb_w", wb_words, N)
        wb_sc = load_scales(second_planes, O + N, wb_scales, N)
        put_p = load_list("put_p", offs7)

        pw = [keep.tile([P, C], F32, name="pw%d" % t) for t in range(PACK)]
        pv = [keep.tile([P, C], F32, name="pv%d" % t) for t in range(PACK)]

        w_w = keep.tile([P, PACK, 2 * P], U8, name="w_w", align_bytes=64)
        nc.vector.tensor_copy(w_w[:].bitcast(U16), w_raw[:].bitcast(U16).rearrange("p (m t) -> p t m", t=PACK))

        def pick(name, table, offsets, dtype, tag):
            picked = keep.tile([P, J], dtype, name=name, tag=tag, align_bytes=64)
            nc.vector.tensor_copy(picked[:], table[:].indirect(offsets[:]))
            return picked

        def first_product(sums, picked_w, picked_sc, fmt, order):
            for t in order:
                nc.tensor.matmul_mx(
                    out=sums[t],
                    lhsT=w_w[:, t, :].bitcast(E2M1),
                    lhsT_scale=w_sc[t][:],
                    rhs=picked_w[:].bitcast(fmt),
                    rhs_scale=picked_sc[:],
                    start=True,
                    stop=True,
                )

        a_sb = [keep.tile([P, J], F32, name="a_sb%d" % t, tag="a_sb%d" % t, align_bytes=64) for t in range(PACK)]
        b_sb = [keep.tile([P, 2, J], F32, name="b_sb%d" % u) for u in range(2)]
        got_a = [keep.tile([P, O], F32, name="got_a%d" % t) for t in range(PACK)]
        diff = [keep.tile([P, 2, O], F32, name="diff%d" % u) for u in range(2)]

        def place(board, values, offsets, t):
            if t < 2:
                nc.vector.tensor_copy(board[t][:].indirect(offsets[:]), values)
            else:
                nc.scalar.activation(board[t][:].indirect(offsets[:]), values, ACT.Copy)

        tok_sc = pick("tok_sc", xt_sc, tok_list, U8, "picked_sc")
        tok_w = pick("tok_w", xt_w, tok_list, U32, "picked_w")
        w_sc = [keep.tile([P, P], U8, name="w_sc%d" % t, align_bytes=64) for t in range(PACK)]
        for t in (0, 2, 1, 3):
            nc.vector.tensor_copy(w_sc[t][:], w_raw_sc[:, t::PACK])
        a_banks = [psum.tile([P, J], F32, name="a_bank%d" % t, tag="bank%d" % t) for t in range(PACK)]
        first_product([bank[:] for bank in a_banks], tok_w, tok_sc, E5M2, (0, 2, 1, 3))
        for t in (0, 2, 1, 3):
            nc.vector.memset(pw[t][:], 0.0)
        for t in range(PACK):
            nc.vector.memset(pv[t][:], 0.0)
        page0 = keep.tile([P, E], F32, name="page0", tag="w_raw_sc", align_bytes=64)
        nc.vector.memset(page0[:], 0.0)
        nc.vector.tensor_copy(a_sb[0][:], a_banks[0][:])
        note_w = pick("note_w", xo_w, note_list, U32, "picked_w")
        note_sc = pick("note_sc", xo_sc, note_list, U8, "picked_sc")
        b_banks = [psum.tile([P, 2, J], F32, name="b_bank%d" % u) for u in range(2)]
        first_product([b_banks[t // 2][:, t % 2, :] for t in range(PACK)], note_w, note_sc, E4M3, range(PACK))
        place(pw, a_sb[0][:], put_a, 0)
        nc.vector.tensor_copy(a_sb[1][:], a_banks[1][:])
        place(pw, a_sb[1][:], put_a, 1)
        for t in (2, 3):
            nc.scalar.copy(a_sb[t][:], a_banks[t][:])
            place(pw, a_sb[t][:], put_a, t)
        for u in range(2):
            nc.scalar.copy(b_sb[u][:], b_banks[u][:])
        for t in (0, 1):
            place(pv, b_sb[t // 2][:, t % 2, :], put_b, t)
        for t in range(PACK):
            nc.scalar.activation(got_a[t][:], pw[t][:].indirect(read_a[:]), ACT.Copy)
        for t in (2, 3):
            place(pv, b_sb[t // 2][:, t % 2, :], put_b, t)
        for t in range(PACK):
            nc.vector.tensor_tensor(diff[t // 2][:, t % 2, :], pv[t][:].indirect(read_b[:]), got_a[t][:], ALU.subtract)

        p_banks = [psum.tile([P, O], F32, name="p_bank%d" % h) for h in range(N // P)]
        for h in range(N // P):
            nc.tensor.matmul_mx(
                out=p_banks[h][:],
                lhsT=ws_w[:, 2 * P * h : 2 * P * (h + 1)].bitcast(E2M1),
                lhsT_scale=ws_sc[:, P * h : P * (h + 1)],
                rhs=sx_w[:].bitcast(E4M3),
                rhs_scale=sx_sc[:],
                start=True,
                stop=False,
            )

        hid = keep.tile([P, O, PACK], BF16, name="hid", tag="hid", align_bytes=64)
        def magnitude_on_scalar(u, cols):
            nc.scalar.activation(
                hid[:, cols, 2 * u : 2 * u + 2].rearrange("p (c i) t -> p c t i", i=4),
                diff[u][:, :, cols].rearrange("p t (c i) -> p c t i", i=4),
                ACT.Abs,
            )

        magnitude_on_scalar(0, slice(0, O))
        magnitude_on_scalar(1, slice(0, O // 2))
        upper = diff[1][:, :, O // 2 :].rearrange("p t o -> p o t")
        nc.vector.scalar_tensor_tensor(hid[:, O // 2 :, 2:4], upper, -1.0, upper, ALU.mult, ALU.max)
        hid_w = keep.tile([P, O], U32, name="hid_w", align_bytes=64)
        hid_sc = keep.tile([P, O], U8, name="hid_sc", align_bytes=64)
        nc.vector.quantize_mx(out=hid_w[:].bitcast(E4M3), scales=hid_sc[:], in_=hid[:].rearrange("p o t -> p (o t)"))

        page1 = keep.tile([P, E], F32, name="page1", tag="hid", align_bytes=64)
        nc.vector.memset(page1[:], 0.0)
        pages = [page0, page1]
        p_sb = [keep.tile([P, O], F32, name="p_sb%d" % h) for h in range(N // P)]
        for h in range(N // P):
            nc.tensor.matmul_mx(
                out=p_banks[h][:],
                lhsT=wb_w[:, 2 * P * h : 2 * P * (h + 1)].bitcast(E2M1),
                lhsT_scale=wb_sc[:, P * h : P * (h + 1)],
                rhs=hid_w[:].bitcast(E4M3),
                rhs_scale=hid_sc[:],
                start=False,
                stop=True,
            )
        nc.vector.tensor_copy(p_sb[0][:], p_banks[0][:])
        nc.vector.tensor_copy(pages[0][:].indirect(put_p[:]), p_sb[0][:])
        nc.sync.dma_start(out[0:P, :], pages[0][:])
        nc.scalar.copy(p_sb[1][:], p_banks[1][:])
        nc.scalar.activation(pages[1][:].indirect(put_p[:]), p_sb[1][:], ACT.Copy)
        nc.sync.dma_start(out[P : 2 * P, :], pages[1][:])
